import numpy as np, ml_dtypes
CORES = [8,136,40,168]
N = 4
BF = ml_dtypes.bfloat16
W, LN, HO, TH = 2048, 256, 7, 67
def spot(a, s, k):
    return ((a * s >> 5) + a + 37 * s + k) & (W - 1)
def parts(rng):
    return (rng.integers(0, 16, (N, 8, 16, W)), rng.integers(0, W, (N, 8, 16, LN)), rng.integers(0, 16, (N, 8, 16, LN)), rng.integers(0, 16, (N, 8, 16, LN)),
            rng.integers(0, W, (N, 8, LN)), rng.integers(0, W, (N, 8, 16)))
def pack(X, P, A, R, s, K):
    b = lambda v, n: np.ascontiguousarray(np.reshape(v, (N, 128, n))).astype(np.float32).astype(BF)
    return {"x": b(X, W), "pn": np.ascontiguousarray(P.reshape(N, 128, LN)).astype(np.int32), "a0": b(A, LN), "r0": b(R, LN),
            "s0": np.ascontiguousarray(s).astype(np.int32), "kap": np.ascontiguousarray(K.reshape(N, 128, 1)).astype(np.int32)}
def setup_inputs(rng):
    return pack(*parts(rng))
def setup_inputs_spread(rng):
    X, P, A, R, s, K = parts(rng); lg = W.bit_length() - 1
    def small(n):
        top = rng.integers(0, 16, (N, 8, 1, n)); return np.minimum((rng.random((N, 8, 16, n)) * (top + 1)).astype(np.int64), top)
    def skew(*sh):
        v = np.minimum(np.exp2(lg * rng.random(sh)).astype(np.int64) - 1, W - 1); return np.where(rng.random(sh) < 0.5, v, W - 1 - v)
    X, P, A, R, s, K = small(W), skew(N, 8, 16, LN), small(LN), small(LN), skew(N, 8, LN), skew(N, 8, 16)
    pairs = ((3, 21), (21, 3), (5, 19), (19, 5), (7, 9), (9, 7))
    for q in range(N):
        for g in range(0, 8, 2):
            u, v = pairs[int(rng.integers(0, 6))]; l = int(rng.integers(0, LN))
            s[q, g, l] = W - u; K[q, g] = (W - v - spot(P[q, g, :, l], W - u, 0)) & (W - 1)
    return pack(X, P, A, R, s, K)
def setup_inputs_ends(rng):
    e = W - 1; bit = lambda *sh: rng.integers(0, 2, sh)
    def ends(n):
        v = 15 * bit(N, 8, 16, n); return np.where(rng.random((N, 8, 1, n)) < 0.5, v[:, :, :1], v)
    X, A, R = ends(W), ends(LN), ends(LN); P, s, K = e * bit(N, 8, 16, LN), e * bit(N, 8, LN), e * bit(N, 8, 16)
    K[:, :, 15] = 0; K[:, :, 14] = e
    for l in (0, 1, 6, LN - 2, LN - 1): P[..., l] = e; s[..., l] = e
    s[..., 3] = 0; s[..., LN - 3] = 0
    lo = sorted(set(spot(a, 0, k) for a in (0, e) for k in (0, e))); hi = sorted(set(spot(a, e, k) for a in (0, e) for k in (0, e)))
    w = bit(N, 8, 1, 1); o = rng.permutation(N - 1)
    for q, far in ((N - 1, 1), (int(o[0]), 0), (int(o[1]), 1)):
        X[q][:, :, lo] = 15 * w[q]; X[q][:, :, hi] = 15 * (1 - w[q])
        A[q] = 15 * ((w[q] + (s[q][:, None, :] > 0) + far) & 1)
    c = int(o[1]); A[c, 7, :, LN - 1] = 15 - A[c, 7, :, LN - 1]
    return pack(X, P, A, R, s, K)
def setup_inputs_corners(rng):
    X, P, A, R, s, K = parts(rng); off = int(rng.integers(0, 4)); H = W // 2; row = np.arange(16)[:, None]
    for q in range(N):
        for g in range(8):
            m = (q + g + off) % 4
            if m == 0:
                c = rng.integers(0, 16, (16, 1)); X[q, g] = c; A[q, g] = c; R[q, g] = c
            elif m == 1:
                c = 15 * int(rng.integers(0, 2)); X[q, g] = c; A[q, g] = 15 - c; R[q, g] = 15 - c
                if g >= 4:
                    s[q, g] = int(rng.integers(0, 32)); P[q, g, 0] = rng.permutation(H)[:LN]
            elif m == 2:
                c = 15 * int(rng.integers(0, 2)); X[q, g, :, :H] = c; X[q, g, :, H:] = 15 - c; A[q, g] = c; R[q, g] = np.where(rng.random(LN) < 0.5, c, 15 - c)
                kind = rng.integers(0, 8, LN); kind[:8] = np.arange(8); kind[LN - 8:] = rng.permutation(8)
                rows = row + np.zeros((1, LN), np.int64)
                mk = np.stack([rows < 0, rows == 0, rows == 15, (rows == 0) | (rows == 15), rows < 15, rows == rng.integers(0, 16, (1, LN)), rows >= 0, rows == 14])
                near = mk[kind, :, np.arange(LN)].T
                site = np.where(rng.random((16, LN)) < 0.3, (H - 1) * rng.integers(0, 2, (16, LN)), rng.integers(0, H, (16, LN))) + np.where(near, 0, H)
                s[q, g] = 0; P[q, g] = (site - K[q, g][:, None]) & (W - 1)
            else:
                s[q, g] = rng.choice(np.array([0, 1, H, W - 1]), LN); K[q, g] = (W - 1) * rng.integers(0, 2, 16)
                P[q, g] = np.where(rng.random((16, LN)) < 0.4, s[q, g][None, :], (W - 1) * rng.integers(0, 2, (16, LN)))
    return pack(X, P, A, R, s, K)
def setup_inputs_crowd(rng):
    X, P, A, R, s, K = parts(rng); h = LN // 2
    P[:, 3] = P[:, 3, :1]
    P[:, ::2] = P[:, ::2, :, :1].copy(); s[:, ::2] = s[:, ::2, :1].copy()
    P[:, 1:7:2, :, h:] = P[:, 1:7:2, :, :h][..., ::-1].copy(); s[:, 1:7:2, h:] = s[:, 1:7:2, :h][..., ::-1].copy()
    P[:, 7, :, 1::2] = P[:, 7, :, ::2].copy(); s[:, 7, 1::2] = s[:, 7, ::2].copy()
    for g in (0, 6):
        A[:, g] = rng.integers(8, 16, (N, 16, LN))
        for q in range(N): X[q, g][:, spot(P[q, g, :, 0], s[q, g, 0], K[q, g])] = 0
    return pack(X, P, A, R, s, K)
def gaps(rng):
    n = np.where(rng.random((N, 8, 1, LN)) < 0.4, TH - 1, TH + rng.integers(0, 17, (N, 8, 1, LN))); n[..., 0] = TH; n[..., LN - 1] = TH - 1
    return n
def dist(rng, z, n):
    i = np.argsort(rng.random((N, 8, 16, LN)), axis=2)
    return np.abs(z - ((n + i) >> 4))
def setup_inputs_ties(rng):
    X, P, A, R, s, K = parts(rng)
    z = 15 * rng.integers(0, 2, (N, 8, 1, W)); z[:, ::2] = z[:, ::2, :, :1].copy()
    zl = 15 * rng.integers(0, 2, (N, 8, 1, LN)); zl[:, ::2] = z[:, ::2, :, :1]
    c = int(rng.integers(0, N)); b = (c - 1) % N; a = (c - 2) % N
    zc = 15 * ((np.arange(8) // 2 + int(rng.integers(0, 2))) & 1)[:, None, None]
    z[c] = zc
    for q in (a, b): z[q, ::2] = zc[::2]
    for q in (a, b, c): zl[q] = zc
    na, nr = gaps(rng), gaps(rng)
    na[b] = TH - 1; nr[b] = TH - 1; na[c] = TH - 1; na[c, :, 0, 0] = TH
    e = int(rng.integers(1, 8)); gs = rng.integers(0, 8, e); ls = 1 + rng.permutation(LN - 2)[:e]
    na[c, gs, 0, ls] = TH + rng.integers(0, 17, e)
    X[:] = z
    return pack(X, P, dist(rng, zl, na), dist(rng, zl, nr), s, K)
def check_inputs(d):
    bad = []
    for k, lo, hi in (("x", 0, 15), ("pn", 0, W - 1), ("a0", 0, 15), ("r0", 0, 15), ("s0", 0, W - 1), ("kap", 0, W - 1)):
        v = np.asarray(d[k]).astype(np.float64)
        if not np.all((v >= lo) & (v <= hi) & (v == np.floor(v))): bad.append("range of " + k)
    return bad
def reference(x, pn, a0, r0, s0, kap):
    X = x.astype(np.float32).astype(np.int64).reshape(N, 8, 16, W); P = pn.astype(np.int64).reshape(N, 8, 16, LN)
    A = a0.astype(np.float32).astype(np.int64).reshape(N, 8, 16, LN); R = r0.astype(np.float32).astype(np.int64).reshape(N, 8, 16, LN)
    s = s0.astype(np.int64); K = kap.astype(np.int64).reshape(N, 8, 16, 1)
    p = np.zeros((N, 8, LN), np.int64); ex = np.zeros((N, 8, LN), np.int64); missed = np.zeros(N, np.int64); row = np.arange(16)[:, None]
    for t in range(HO):
        last = missed; missed = np.zeros(N, np.int64)
        for r in range(N):
            q = (r + t) % N
            h = spot(P[r], s[r][:, None, :], K[q])
            v = np.take_along_axis(X[q], h.reshape(8, 1, 16 * LN), 2).reshape(8, 16, 16, LN)
            dd = np.add.reduce(np.abs(v - A[r][:, :, None, :]), axis=1)
            near = (dd < TH + (last[q] & 15)) & (row >= p[r][:, None, :]); hit = np.any(near, axis=1)
            k = np.where(hit, 15 - np.argmax(near[:, ::-1], axis=1), p[r])
            hk = np.take_along_axis(h, k[:, None, :], 1)[:, 0]
            back = ((s[r] * hk >> 5) + s[r] + 811 * t) & (W - 1)
            new = np.where((row >= p[r][:, None, :]) & (row <= k[:, None, :]), back[:, None, :], P[r])
            turn = ~hit | (k == 15); tu = turn[:, None, :]
            for g in range(8):
                m = np.flatnonzero(~hit[g]); place, first = np.unique(hk[g][m], return_index=True); lane = m[first]
                X[q, g][:, place] = (X[q, g][:, place] + A[r, g][:, lane]) >> 1
            missed[q] = np.count_nonzero(~hit)
            P[r] = np.where(tu, new[:, ::-1], new); p[r] = np.where(turn, 15 - k, k + 1); s[r] = hk; ex[r] = ex[r] ^ turn
            A[r], R[r] = np.where(tu, R[r], A[r]), np.where(tu, A[r], R[r])
    at = [(q - (HO - 1)) % N for q in range(N)]
    return {"yn": P[at].reshape(N, 128, LN).astype(np.float32), "ys": s[at].astype(np.float32), "yp": (p[at] + 16 * ex[at]).astype(np.float32),
            "yx": X.reshape(N, 128, W).astype(np.float32).astype(BF)}

from concourse.mybir import AluOpType, AxisListType, ActivationFunctionType

A_ = AluOpType
F_ = ActivationFunctionType
HOPS = 7
NX = 2080
RELU = 1

SCRATCH = {}
PART = {}
for _b, _d, _w, _ns in (("f32s", "float32", 16, ("so", "y1", "po", "jk", "ge", "pa", "pb", "G", "Fv", "hg", "tt", "sC", "U2", "KD")),
                        ("i32s", "int32", 16, ("ip", "inn", "il", "irv", "idl", "CI", "li", "rvi", "kl", "hs", "W2", "v2", "tb", "qq", "bb", "pq"))):
    SCRATCH[_b] = ("sbuf", [128, _w * len(_ns)], _d)
    for _k, _n in enumerate(_ns):
        PART[_n] = (_b, _w * _k, 8 if _n in ("ge", "pa", "pb", "idl") else _w)


def _sb(n, w, d):
    if n not in PART:
        SCRATCH[n] = ("sbuf", [128, w], d)


for _n, _w, _d in (
    ("X", NX, "bfloat16"), ("AR", 2048, "bfloat16"), ("DR", 4096, "bfloat16"), ("DA", 4096, "bfloat16"),
    ("LE", 2048, "bfloat16"), ("LP", 2048, "bfloat16"), ("L2", 2048, "bfloat16"), ("KI", 2048, "bfloat16"), ("KU", 256, "bfloat16"), ("DG", 2048, "float16"),
    ("MC", 48 * HOPS, "float16"), ("MP", 256 * HOPS, "float16"), ("CO", 48 * HOPS, "float16"), ("PO", 256 * HOPS, "float16"),
    ("PI", 256, "int32"), ("SI", 16, "int32"), ("KA", 1, "int32"),
    ("ia", 128, "int32"), ("ib", 128, "int32"), ("ip", 16, "int32"), ("inn", 16, "int32"), ("il", 16, "int32"),
    ("idl", 8, "int32"), ("irv", 16, "int32"), ("DUM", 16, "int32"), ("bmi", 128, "int32"), ("CI", 16, "int32"),
    ("li", 16, "int32"), ("ge", 8, "float32"), ("pa", 8, "float32"), ("pb", 8, "float32"), ("rvi", 16, "int32"),
    ("Ib", 128, "bfloat16"), ("NI", 128, "bfloat16"), ("I4k", 128, "bfloat16"), ("N4k", 128, "bfloat16"),
    ("NB", 128, "bfloat16"), ("N128", 128, "bfloat16"), ("N2k", 128, "bfloat16"), ("If", 128, "float16"),
    ("I16", 128, "float16"), ("I32", 128, "float16"), ("I1184", 128, "float16"), ("BM", 128, "bfloat16"), ("BMf", 128, "float16"),
    ("B8", 8, "bfloat16"), ("ONE", 512, "bfloat16"), ("Z0", 128, "bfloat16"), ("F25", 128, "bfloat16"), ("F376", 128, "bfloat16"),
    ("Fm256", 128, "bfloat16"), ("Fm", 128, "bfloat16"), ("F16", 128, "bfloat16"),
    ("REP", 16, "uint16"), ("RK", 16, "uint16"), ("RVK", 16, "uint16"), ("RVP", 16, "uint16"), ("PRE", 8, "uint16"), ("PRL", 8, "uint16"),
    ("SEL", 16, "float16"), ("LT", 16, "float16"), ("kf", 1, "float32"), ("rk", 16, "float16"), ("KC", 16, "float32"),
    ("KTa", 256, "float16"), ("KTb", 256, "float16"), ("KD", 16, "float32"),
    ("TH", 128, "bfloat16"), ("AO", 16, "uint16"), ("AC", 256, "bfloat16"), ("T1", 256, "bfloat16"), ("I64k", 128, "bfloat16"),
    ("Z", 256, "float32"), ("ZI", 256, "int32"), ("HI", 256, "int32"), ("H16", 256, "uint16"), ("HK", 256, "float32"), ("FL", 256, "float32"),
    ("M", 64, "float32"), ("M2", 32, "float32"), ("Wv", 16, "int32"), ("kl", 16, "int32"), ("kc", 16, "float16"), ("hs", 16, "int32"),
    ("W2", 16, "int32"), ("tt", 16, "float32"), ("v2", 16, "int32"), ("hg", 16, "float32"), ("tb", 16, "int32"), ("qq", 16, "int32"),
    ("bb", 16, "int32"), ("b16", 16, "float16"), ("pq", 16, "int32"), ("sC", 16, "float32"), ("U2", 16, "float32"),
    ("hu", 16, "uint16"), ("hit", 16, "bfloat16"), ("key", 16, "float32"), ("KL", 128, "float32"), ("eq", 128, "bfloat16"),
    ("G", 16, "float32"), ("Fv", 16, "float32"), ("FT", 128, "float16"), ("fo", 32, "uint16"), ("old", 256, "bfloat16"),
    ("nv", 256, "int32"), ("R2", 256, "bfloat16"), ("tP", 256, "float16"), ("jk", 16, "float32"), ("mc", 1, "float32"),
    ("mi", 1, "int32"), ("mj", 1, "int32"), ("mt", 1, "float32"),
    ("Pf", 256, "float32"), ("Pv", 256, "float32"), ("ya", 256, "float32"), ("yb", 256, "float32"), ("yo", 256, "float32"),
    ("so", 16, "float32"), ("y1", 16, "float32"), ("po", 16, "float32"),
):
    _sb(_n, _w, _d)
PS = ("E0", "E1", "Q0", "Q1", "SK", "CC", "RG", "OB")
for _n in PS:
    SCRATCH[_n] = ("psum", [128, 512], "float32")

SEMAPHORES = (["qv", "qs", "qp", "qg", "snd", "lx", "la", "lr", "lk", "lz", "lpy", "lps", "oy", "oz"]
              + ["mc%d" % t for t in range(1, HOPS)] + ["mp%d" % t for t in range(1, HOPS)] + ["ar%d" % d for d in (1, 2, 3)])


def rank_program(g, core, T, topo):
    rank = T.rank_of(core)
    if rank is None:
        return
    n = len(T.cores)
    nxt, prv = T.cores[(rank + 1) % n], T.cores[(rank - 1) % n]
    Q = {"v": g.vector, "s": g.scalar, "p": g.tensor, "g": g, "y": g.sync}
    QS = {"v": "qv", "s": "qs", "p": "qp", "g": "qg"}
    cnt = {q: 0 for q in Q}
    seen = {q: {} for q in Q}
    log = {}
    sent = [0]

    def view(name, a=0, b=None, st=1):
        if name in PART:
            name, o, w = PART[name]
            a, b = o + a, o + (w if b is None else b)
        b = SCRATCH[name][1][1] if b is None else b
        ap = T[name][:, a:b] if st == 1 else T[name][:, a:b:st]
        return (ap, name, a, b)

    def need(q, ev):
        if seen[q].get(ev[0], 0) < ev[1]:
            seen[q][ev[0]] = ev[1]
            Q[q].wait_ge(T.sem[ev[0]], ev[1])

    def order(q, outs, ins):
        todo = {}
        for vs, wr in ((ins, False), (outs, True)):
            for _, nm, a, b in vs:
                ps = nm in PS
                for (q2, a2, b2, w2), ev in log.get(nm, {}).items():
                    hitx = a < b2 and a2 < b
                    dep = (hitx and w2 and not (wr and ps)) or (q2 != q and ((hitx and (wr or w2)) or ps))
                    if dep and todo.get(ev[0], 0) < ev[1]:
                        todo[ev[0]] = ev[1]
        for k in sorted(todo):
            need(q, (k, todo[k]))

    def note(q, outs, ins, ev):
        for vs, wr in ((ins, False), (outs, True)):
            for _, nm, a, b in vs:
                d = log.setdefault(nm, {})
                if wr and nm not in PS:
                    for k in [k for k in d if a <= k[1] and k[2] <= b]:
                        del d[k]
                d[(q, a, b, wr)] = ev

    def emit(q, fn, outs, ins):
        order(q, outs, ins)
        cnt[q] += 1
        fn().then_inc(T.sem[QS[q]], 1)
        note(q, outs, ins, (QS[q], cnt[q]))

    def tt(o, a, b, op):
        emit("v", lambda: g.vector.tensor_tensor(o[0], a[0], b[0], op), [o], [a, b])

    def tti(o, win, off, b, op):
        emit("v", lambda: g.vector.tensor_tensor(o[0], win[0].indirect(off[0]), b[0], op), [o], [win, off, b])

    def ts(o, a, s1, op0, s2=None, op1=None):
        col = isinstance(s1, tuple)
        sc = s1[0] if col else s1
        if op1 is None:
            f = lambda: g.vector.tensor_scalar(o[0], a[0], sc, None, op0)
        else:
            f = lambda: g.vector.tensor_scalar(o[0], a[0], sc, s2, op0, op1)
        emit("v", f, [o], [a] + ([s1] if col else []))

    def cp(o, a):
        emit("v", lambda: g.vector.tensor_copy(o[0], a[0]), [o], [a])

    def cpi(o, win, off):
        emit("v", lambda: g.vector.tensor_copy(o[0], win[0].indirect(off[0])), [o], [win, off])

    def scat(win, off, a):
        emit("v", lambda: g.vector.tensor_copy(win[0].indirect(off[0]), a[0]), [win], [off, a])

    def ms(o, c):
        emit("v", lambda: g.vector.memset(o[0], c), [o], [])

    def act(o, a, f=F_.Copy, scale=1.0):
        if isinstance(scale, tuple):
            emit("s", lambda: g.scalar.activation(o[0], a[0], f, scale=scale[0]), [o], [a, scale])
        else:
            emit("s", lambda: g.scalar.activation(o[0], a[0], f, scale=scale), [o], [a])

    def acti(o, win, off):
        emit("s", lambda: g.scalar.activation(o[0], win[0].indirect(off[0]), F_.Copy), [o], [win, off])

    def mm(o, l, r, start, stop):
        emit("p", lambda: g.tensor.matmul(o[0], l[0], r[0], start, stop), [o], [l, r])

    def iota(nm, pat, base, cm):
        o = view(nm)
        emit("g", lambda: g.iota(o[0], pat, base, cm), [o], [])

    def load(q, o, src, sem, total=16):
        order(q, [o], [])
        Q[q].dma_start(o[0], src).then_inc(T.sem[sem], 16)
        note("dma", [o], [], (sem, total))

    def send(dst, o, a, sem):
        order("g", [], [a])
        rid, pid = topo.addr(dst, core)
        g.remote_dma(o[0], a[0], T.sem[sem], T.sem.snd, pid, rid, topo.mask(core, dst))
        sent[0] += len(topo.engines(core, dst))

    load("y", view("SI"), T.s0[:], "lz")
    load("s", view("KA"), T.kap[:], "lk")
    for k in range(16):
        q, sem = (("y", "lpy"), ("s", "lps"))[k % 2]
        load(q, view("PI", 16 * k, 16 * k + 16), T.pn[k::16, :], sem, 128)
    load("y", view("AR", 0, 256), T.a0[:], "la")
    load("s", view("AR", 256, 512), T.r0[:], "lr")
    load("y", view("X", 0, 2048), T.x[:], "lx")

    iota("ia", [[-1, 128]], 0, 1)
    iota("ib", [[-16, 8], [0, 16]], 0, 1)
    iota("ip", [[0, 16]], 0, 1)
    iota("inn", [[1, 16]], 0, 0)
    iota("il", [[1, 16]], 0, 16)
    iota("irv", [[-16, 16]], 240, 0)
    iota("idl", [[1, 8]], 1, 0)
    iota("DUM", [[2, 16]], 2048, 0)
    ts(view("Ib"), view("ia"), 0, A_.is_equal)
    ts(view("If"), view("ia"), 0, A_.is_equal)
    ts(view("bmi"), view("ib"), 4, A_.arith_shift_right)
    ts(view("CI"), view("ip"), 15, A_.bitwise_and)
    ts(view("li"), view("il"), 255, A_.bitwise_and)
    ts(view("BM"), view("bmi"), 0, A_.is_equal)
    ts(view("BMf"), view("bmi"), 0, A_.is_equal)
    tt(view("SEL"), view("CI"), view("inn"), A_.is_equal)
    cp(view("REP"), view("CI"))
    cp(view("RK"), view("inn"))
    ts(view("RVK"), view("inn"), -1, A_.mult, 15, A_.add)
    ts(view("LT"), view("li"), 128, A_.add)
    ms(view("ONE"), 1.0)
    ms(view("F25"), 0.25)
    ts(view("I32"), view("If"), 32.0, A_.mult)
    ts(view("I16"), view("If"), 16.0, A_.mult)
    ts(view("I1184"), view("If"), 1184.0, A_.mult)
    for nm, c in (("NI", -1.0), ("N128", -128.0), ("I4k", 4096.0), ("N4k", -4096.0), ("NB", -262144.0), ("N2k", -2048.0), ("I64k", 65536.0)):
        act(view(nm), view("Ib"), scale=c)
    for k in range(16):
        act(view("KI", 128 * k, 128 * k + 128), view("Ib"), scale=7.5 - k)
    cp(view("kf"), view("KA"))
    ts(view("rk"), view("SEL"), view("kf"), A_.mult)
    mm(view("Q1", 0, 16), view("BMf"), view("rk"), True, True)
    cp(view("KC"), view("Q1", 0, 16))
    cpi(view("KTa"), view("KC"), view("RK"))
    cpi(view("KTb"), view("KC"), view("RVK"))
    ms(view("F376"), 376.0)
    ms(view("Fm256"), -256.0)
    ms(view("TH"), 67.0 * 512)
    ms(view("LE"), 0.0)
    ts(view("B8"), view("BM", 0, 128, 16), -65536.0, A_.mult)
    for i in range(16):
        cp(view("LE", 128 * i + i, 128 * i + 128, 16), view("B8"))
    ms(view("Z0"), 0.0)
    ms(view("Fm"), -1.0 / 4096)
    ms(view("F16"), 16.0)
    tt(view("ge"), view("CI", 0, 8), view("idl"), A_.is_ge)
    ts(view("pb"), view("idl"), -1, A_.mult, 16, A_.add)
    tt(view("rvi"), view("irv"), view("CI"), A_.add)
    tt(view("pa"), view("ge"), view("idl"), A_.mult)
    ts(view("ge"), view("ge"), -1, A_.mult, 1, A_.add)
    cp(view("RVP"), view("rvi"))
    tt(view("pa"), view("CI", 0, 8), view("pa"), A_.subtract)
    tt(view("pb"), view("pb"), view("ge"), A_.mult)
    tt(view("KD"), view("KTa", 0, 256, 16), view("KTb", 0, 256, 16), A_.subtract)
    cp(view("PRE"), view("pa"))
    tt(view("pb"), view("CI", 0, 8), view("pb"), A_.add)
    for k in range(16):
        ts(view("DG", 128 * k, 128 * k + 128), view("I16"), view("KD", k, k + 1), A_.mult)
    cp(view("PRL"), view("pb"))
    cp(view("MC", 0, 16), view("SI"))
    ts(view("MC", 16, 32), view("inn"), 0, A_.mult, 1, A_.add)
    ts(view("MC", 32, 48), view("inn"), 0, A_.mult, -7.5, A_.add)
    cp(view("MP", 0, 256), view("PI"))
    for d in (1, 2, 3):
        send(T.cores[(rank + d) % n], view("AR", 512 * d, 512 * d + 512), view("AR", 0, 512), "ar%d" % d)

    outs = {}

    def store(q, out, a, sem):
        order(q, [], [a])
        Q[q].dma_start(out, a[0]).then_inc(T.sem[sem], 16)
        outs[sem] = outs.get(sem, 0) + 16

    def finish_names(U):
        acti(view("Pv"), view("Pf"), view("RVP"))
        mm(view("SK", 0, 256), view("F16"), view("ONE", 0, 256), True, False)
        for k in range(16):
            mm(view("SK", 16 * k, 16 * k + 16), view("N2k"), U, False, k == 15)
        ts(view("y1"), U, -8.0, A_.mult, 8.0, A_.add)
        cp(view("so"), view("hs"))
        tt(view("po"), view("pq"), view("y1"), A_.add)
        tt(view("yb"), view("Pf"), view("SK", 0, 256), A_.subtract)
        tt(view("SK", 0, 256), view("Pv"), view("SK", 0, 256), A_.min)
        tt(view("yo"), view("SK", 0, 256), view("yb"), A_.max)
        for k in range(16):
            store(("y", "s")[k % 2], T.yn[k::16, :], view("yo", 16 * k, 16 * k + 16), ("oy", "oz")[k % 2])
        store("y", T.ys[:], view("so"), "oy")
        store("s", T.yp[:], view("po"), "oz")

    for t in range(HOPS):
        last = t == HOPS - 1
        s_, U, pc = (view("MC", 48 * t + 16 * x, 48 * t + 16 * x + 16) for x in range(3))
        P = view("MP", 256 * t, 256 * t + 256)
        if t:
            ne = len(topo.engines(prv, core))
            note("rem", [view("MC", 48 * t, 48 * t + 48)], [], ("mc%d" % t, ne))
            note("rem", [P], [], ("mp%d" % t, ne))
        d = t % n
        if 1 <= t <= 3:
            note("rem", [view("AR", 512 * d, 512 * d + 512)], [], ("ar%d" % d, len(topo.engines(T.cores[(rank - d) % n], core))))
        mm(view("OB", 256, 512), view("F25"), view("ONE", 0, 256), True, False)
        if t:
            mm(view("SK", 256, 512), view("I16"), view("KTa"), True, False)
            mm(view("SK", 256, 512), view("I16"), view("KTb"), False, False)
        else:
            mm(view("SK", 256, 512), view("I32"), view("KTa"), True, False)
        mm(view("Q0", 0, 16), view("N128"), U, True, False)
        mm(view("Q0", 0, 16), view("If"), view("LT"), False, True)
        cp(view("AO"), view("Q0", 0, 16))
        acti(view("AC"), view("AR", 512 * d, 512 * d + 512), view("AO"))
        for k in range(16):
            mm(view("OB", 256 + 16 * k, 272 + 16 * k), view("If"), s_, False, k == 15)
        for k in range(16):
            o = view("SK", 256 + 16 * k, 272 + 16 * k)
            if t:
                mm(o, view("DG", 128 * k, 128 * k + 128), U, False, False)
            mm(o, view("I1184"), s_, False, k == 15)
        for k in range(16):
            mm(view("RG", 256 + 16 * k, 272 + 16 * k), view("KI", 128 * k, 128 * k + 128), U, True, True)
        act(view("KU"), view("RG", 256, 512))
        ts(view("sC"), s_, 32.0, A_.mult, 25952.0 * t, A_.add)
        ts(view("U2"), U, 2.0, A_.mult)
        for a in (0, 128):
            b = a + 128
            tt(view("Z", a, b), view("MP", 256 * t + a, 256 * t + b), view("OB", 256 + a, 256 + b), A_.mult)
            tt(view("ZI", a, b), view("Z", a, b), view("SK", 256 + a, 256 + b), A_.add)
            ts(view("HI", a, b), view("ZI", a, b), 5, A_.arith_shift_right, 2047, A_.bitwise_and)
            cp(view("H16", a, b), view("HI", a, b))
        mm(view("RG", 0, 256), view("Ib"), view("KU"), True, False)
        for k in range(16):
            mm(view("RG", 16 * k, 16 * k + 16), view("If"), pc, False, k == 15)

        def bounds():
            act(view("T1"), view("RG", 0, 256), F_.Relu)
            mm(view("CC", 0, 256), view("F376"), view("ONE", 0, 256), True, False)
            mm(view("CC", 0, 256), view("N2k"), view("KU"), False, False)
            mm(view("CC", 0, 256), view("NB"), view("T1"), False, True)
            mm(view("CC", 256, 512), view("Fm256"), view("ONE", 0, 256), True, False)
            mm(view("CC", 256, 512), view("I64k"), view("KU"), False, False)
            for k in range(16):
                mm(view("CC", 256 + 16 * k, 272 + 16 * k), view("I64k"), pc, False, k == 15)

        W_ = view("X", 0, 2048)

        def grow(k):
            acti(view("DR", 256 * k, 256 * k + 256), W_, view("H16", 16 * k, 16 * k + 16))

        def psub(c):
            q = "Q%d" % (c % 2)
            mm(view(q, 0, 512), view("Ib"), view("DR", 1024 * c, 1024 * c + 512), True, False)
            mm(view(q, 0, 256), view("NI"), view("AC"), False, False)
            mm(view(q, 256, 512), view("NI"), view("AC"), False, True)

        def vrows(*ks):
            for k in ks:
                tti(view("DR", 256 * k, 256 * k + 256), W_, view("H16", 16 * k, 16 * k + 16), view("AC"), A_.subtract)

        def absps(c):
            act(view("DA", 1024 * c, 1024 * c + 512), view("Q%d" % (c % 2), 0, 512), F_.Abs)

        def absrows(k, k2):
            act(view("DA", 256 * k, 256 * k2), view("DR", 256 * k, 256 * k2), F_.Abs)

        def dsum(c):
            o = view("E%d" % (c % 2), 0, 64)
            mm(o, view("TH"), view("ONE", 0, 64), True, False)
            for nm, src in ((("LP", "DR"), ("L2", "DA")) if c == RELU else (("LE", "DA"),)):
                for i in range(16):
                    mm(o, view(nm, 128 * i, 128 * i + 128), view(src, 1024 * c + i, 1024 * c + 1024, 16), False, i == 15 and nm != "LP")

        def decide(c):
            e = view("E%d" % (c % 2), 0, 64)
            tt(e, e, view("FL", 64 * c, 64 * c + 64), A_.max)
            if c == 0:
                tt(view("M"), e, view("HK", 0, 64), A_.min)
            else:
                tt(e, e, view("HK", 64 * c, 64 * c + 64), A_.min)
                tt(view("M"), e, view("M"), A_.max)

        if t == 0:
            ts(view("LP"), view("LE"), -1.0, A_.mult)
            ts(view("L2"), view("LE"), 2.0, A_.mult)
        grow(0)
        grow(1)
        psub(0)
        vrows(2, 3)
        grow(8)
        bounds()
        absps(0)
        absrows(2, 4)
        dsum(0)
        vrows(4, 5, 6, 7)
        ts(view("DA", 1024, 2048), view("DR", 1024, 2048), 0.0, A_.max)
        grow(9)
        psub(2)
        dsum(1)
        tt(view("HK"), view("HI"), view("CC", 0, 256), A_.add)
        tt(view("FL"), view("HK"), view("CC", 256, 512), A_.add)
        vrows(10, 11)
        grow(12)
        absps(2)
        decide(0)
        decide(1)
        vrows(14)
        grow(13)
        psub(3)
        absrows(10, 12)
        dsum(2)
        vrows(15)
        absps(3)
        absrows(14, 15)
        absrows(15, 16)
        dsum(3)
        mm(view("RG", 256, 512), view("Ib"), view("KU"), True, False)
        mm(view("OB", 0, 256), view("I4k"), view("T1"), True, False)
        mm(view("CC", 0, 256), view("N4k"), view("T1"), True, False)
        decide(2)
        decide(3)
        tt(view("M2"), view("M", 0, 32), view("M", 32, 64), A_.max)
        tt(view("Wv"), view("M2", 0, 16), view("M2", 16, 32), A_.max)
        w = view("Wv")
        sn, Un, pn_ = (view("CO", 48 * t + 16 * x, 48 * t + 16 * x + 16) for x in range(3))
        ts(view("kl"), w, 11, A_.arith_shift_right, 15, A_.bitwise_and)
        ts(view("hs"), w, 2047, A_.bitwise_and)
        ts(view("hit"), w, 32768, A_.is_ge, 4096, A_.mult)
        ts(view("kc"), view("kl"), -7.5, A_.add)
        for k in range(16):
            mm(view("RG", 256 + 16 * k, 272 + 16 * k), view("If"), view("kc"), False, k == 15)
        tt(view("tt"), s_, view("hs"), A_.mult)
        tt(view("key"), view("hs"), view("hit"), A_.add)
        ts(view("W2"), w, 2048, A_.add)
        acti(view("KL"), view("key"), view("PRL"))
        tt(view("tb"), view("tt"), view("sC"), A_.add)
        ts(view("v2"), view("W2"), 10, A_.arith_shift_right, 62, A_.bitwise_and)
        ts(view("bb"), view("tb"), 5, A_.arith_shift_right, 2047, A_.bitwise_and)
        ts(view("hg"), view("v2"), 33, A_.is_gt, -0.5, A_.add)
        cp(view("b16"), view("bb"))
        tt(view("qq"), view("v2"), view("hg"), A_.mult)
        cp(sn, view("hs"))
        ts(view("pq"), view("qq"), 15, A_.bitwise_and)
        tt(Un, view("U2"), view("hg"), A_.mult)
        ts(pn_, view("pq"), -7.5, A_.add)
        act(view("R2"), view("RG", 256, 512), F_.Relu, -1.0)
        for k in range(16):
            if k == 10:
                mm(view("OB", 0, 256), view("I4k"), view("R2"), False, True)
            mm(view("CC", 16 * k, 16 * k + 16), view("If"), view("b16"), False, False)
        mm(view("CC", 0, 256), view("N4k"), view("R2"), False, True)
        if not last:
            send(nxt, view("MC", 48 * t + 48, 48 * t + 96), view("CO", 48 * t, 48 * t + 48), "mc%d" % (t + 1))
        tti(view("eq"), view("key"), view("PRE"), view("KL"), A_.is_equal)
        cp(view("hu"), view("hs"))
        acti(view("old"), W_, view("hu"))
        tt(view("tP"), P, view("OB", 0, 256), A_.min)
        if not last:
            tt(view("PO", 256 * t, 256 * t + 256), view("tP"), view("CC", 0, 256), A_.max)
            send(nxt, view("MP", 256 * t + 256, 256 * t + 512), view("PO", 256 * t, 256 * t + 256), "mp%d" % (t + 1))
        else:
            tt(view("Pf"), view("tP"), view("CC", 0, 256), A_.max)
        mm(view("E0", 0, 16), view("Z0"), view("ONE", 0, 16), True, False)
        for dl in range(1, 9):
            a = 16 * (dl - 1)
            mm(view("E0", dl, 16), view("I4k"), view("eq", a + dl, a + 16), False, dl == 8)
            if dl < 8:
                mm(view("E0", 16 - dl, 16), view("I4k"), view("eq", a, a + dl), False, False)
        mm(view("Q1", 0, 256), view("Ib"), view("old"), True, False)
        mm(view("Q1", 0, 256), view("Ib"), view("AC"), False, True)
        tt(view("G"), view("key"), view("E0", 0, 16), A_.max)
        tt(view("Fv"), view("G"), view("DUM"), A_.min)
        tti(view("FT"), view("Fv"), view("REP", 0, 8), view("BM"), A_.mult)
        mm(view("Q0", 0, 16), view("FT"), view("SEL"), True, True)
        ts(view("nv"), view("Q1", 0, 256), 0.5, A_.mult, -0.25, A_.add)
        if last:
            finish_names(Un)
        cp(view("fo", 0, 32, 2), view("Q0", 0, 16))
        if not last:
            mm(view("E1", 0, 16), view("Fm"), view("hit"), True, True)
            o, i_, m_ = view("jk"), view("E1", 0, 16), view("mc")
            emit("s", lambda: g.scalar.activation(o[0], i_[0], F_.Copy, accum_out=m_[0]), [o, m_], [i_])
        for i in range(15, -1, -1):
            scat(view("X", 0, NX), view("fo", 2 * i, 2 * i + 1), view("nv", i, 256, 16))
            if not last:
                if i == 11:
                    ts(view("mi"), view("mc"), 2048, A_.add)
                if i == 7:
                    ts(view("mj"), view("mi"), 15, A_.bitwise_and)
                if i == 3:
                    ts(view("mt"), view("mj"), 67, A_.add, 512, A_.mult)
        if not last:
            act(view("TH"), view("ONE", 0, 128), F_.Copy, view("mt"))

    store("y", T.yx[:], view("X", 0, 2048), "oy")
    for q in ("v", "s", "p", "g"):
        need("g", (QS[q], cnt[q]))
    for sem in outs:
        need("g", (sem, outs[sem]))
    for sem, val in (("lx", 16), ("la", 16), ("lr", 16), ("lk", 16), ("lz", 16), ("lpy", 128), ("lps", 128), ("snd", sent[0])):
        need("g", (sem, val))
